import numpy as np
import ml_dtypes


def mxq(x, axis, fmt="e4m3"):
    dtype, down = {"e4m3": (ml_dtypes.float8_e4m3fn, 7), "e5m2": (ml_dtypes.float8_e5m2, 14)}[fmt]
    v = np.moveaxis(np.asarray(x, np.float32).astype(ml_dtypes.bfloat16).astype(np.float64), axis, -1)
    blocks = v.reshape(v.shape[:-1] + (-1, 32))
    amax = np.abs(blocks).max(-1, keepdims=True)
    byte = np.maximum(np.where(amax > 0, np.frexp(amax)[1] - 1 + 127, 0) - down, 1)
    scale = np.exp2(byte - 127.0)
    codes = (blocks / scale).astype(np.float32).astype(dtype).astype(np.float64)
    return np.moveaxis((codes * scale).reshape(v.shape), -1, axis)


WIDE = False


def mx_kscale(k):
    if not WIDE:
        return np.ones(k)
    levels = np.array([10, -10, 5, -5, 0])
    if k % 512:
        return np.exp2(np.random.permutation(np.resize(levels, k // 32))).repeat(32)
    a = np.empty((k // 512, 16))
    for p in range(k // 512):
        a[p, :8] = np.random.permutation(np.resize(levels, 8))
        for g in range(8):
            far = levels[np.abs(levels - a[p, g]) >= 10]
            a[p, g + 8] = far[np.random.randint(len(far))]
    return np.exp2(a.ravel()).repeat(32)


def f64(x):
    return np.asarray(x).astype(np.float64)


def striped(idx):
    return np.tile(idx.reshape(-1, 16).T, (8, 1)).astype(np.uint16)


def unstriped(offs):
    return offs[:16].T.reshape(-1).astype(np.int64)


def striped8(idx):
    return np.concatenate([v.reshape(-1, 16).T for v in idx]).astype(np.uint16)


def unstriped8(offs):
    return np.stack([offs[16 * g:16 * g + 16].T.reshape(-1) for g in range(8)]).astype(np.int64)


E2M1 = np.array([0.0, 0.5, 1.0, 1.5, 2.0, 3.0, 4.0, 6.0, -0.0, -0.5, -1.0, -1.5, -2.0, -3.0, -4.0, -6.0])


def pack_weight(w, fmt):
    k, n = w.shape
    w = f64(np.asarray(w, np.float32).astype(ml_dtypes.bfloat16)).reshape(k // 32, 32, n)
    amax = np.abs(w).max(1)
    if fmt == "e4m3":
        byte = np.frexp(amax)[1] - 1 + 127 - 7
    else:
        mant, ex = np.frexp(amax / 6.0)
        byte = np.where(mant > 0.5, ex, ex - 1) + 127
    byte = np.clip(np.where(amax > 0, byte, 1), 1, 254)
    scaled = (w * np.exp2(127.0 - byte)[:, None, :]).reshape(k, n).astype(np.float32)
    by_word = np.ascontiguousarray(scaled.reshape(k // 512, 128, 4, n).transpose(0, 1, 3, 2))
    if fmt == "e4m3":
        words = by_word.astype(ml_dtypes.float8_e4m3fn).view(np.uint8)
    else:
        c = by_word.astype(ml_dtypes.float4_e2m1fn).view(np.uint8) & 0xF
        words = (c[..., 0::2] | (c[..., 1::2] << 4)).reshape(k // 512, 128, 2 * n)
    return np.ascontiguousarray(words), np.ascontiguousarray(byte.astype(np.uint8).reshape(k // 512, 16, n))


def unpack_weight(words, scales, fmt):
    g, _, n = scales.shape
    words = np.ascontiguousarray(words).reshape(g, 128, n, -1)
    if fmt == "e4m3":
        vals = words.view(ml_dtypes.float8_e4m3fn).astype(np.float64)
    else:
        nib = np.empty((g, 128, n, 4), np.uint8)
        nib[..., 0::2] = words & 0xF
        nib[..., 1::2] = words >> 4
        vals = E2M1[nib]
    vals = vals * np.repeat(np.exp2(scales.astype(np.float64) - 127.0), 8, axis=1)[..., None]
    return vals.transpose(0, 1, 3, 2).reshape(g * 512, n)


def pack_table(v):
    words, scales = pack_weight(v, "e4m3")
    return np.concatenate([words.reshape(words.shape[0], -1), scales.reshape(scales.shape[0], -1)], axis=1)


def unpack_table(tab):
    g, t = tab.shape[0], tab.shape[1] // 528
    return unpack_weight(tab[:, :512 * t].reshape(g, 128, t, 4), tab[:, 512 * t:].reshape(g, 16, t), "e4m3")


K, M, T, S = 1536, 256, 2048, 1024


def setup_inputs():
    n = np.random.standard_normal
    s = mx_kscale(K)[:, None]
    return {
        "tab": pack_table(n((K, T)) * s),
        "w": (n((K, M)) / np.sqrt(K) / s).astype(np.float32),
        "wgo": np.repeat(np.random.uniform(0.5, 2.0, (8, S)), 16, axis=0).astype(np.float32),
        "offs": striped(np.random.permutation(T)[:S]),
        "offs2": striped8(np.stack([np.random.permutation(T)[:S] for _ in range(8)])),
    }


def reference(tab, w, wgo, offs, offs2):
    tab_ = unpack_table(tab)[:, unstriped(offs)]
    w_ = mxq(f64(w), 0, "e4m3")
    y = w_.T @ tab_
    place = unstriped8(offs2)[np.arange(M) % 128 // 16]
    out = np.zeros((M, T))
    out[np.arange(M)[:, None], place] = f64(wgo)[np.arange(M) % 128] * (y)
    return out

@@ -1,0 +1,145 @@
+from contextlib import ExitStack
+
+import concourse.mybir as mybir
+
+K, M, T, S = 1536, 256, 2048, 1024
+FLOPS = 2 * K * M * S
+
+F32 = mybir.dt.float32
+BF16 = mybir.dt.bfloat16
+I32 = mybir.dt.int32
+U32 = mybir.dt.uint32
+U16 = mybir.dt.uint16
+U8 = mybir.dt.uint8
+FP8X4 = mybir.dt.float8_e4m3fn_x4
+MULT = mybir.AluOpType.mult
+
+P = 128
+PACK = 4
+K_PASS = P * PACK
+PASSES = K // K_PASS
+M_TILES = M // P
+HALF = 512
+HALVES = S // HALF
+
+
+def tile_list_tabhs_none_kernel(tc, tab, w, wgo, offs, offs2, out):
+    nc = tc.nc
+    with ExitStack() as ctx:
+        lists = ctx.enter_context(tc.tile_pool(name="lists", bufs=1))
+        keep = ctx.enter_context(tc.tile_pool(name="keep", bufs=1))
+        psum = ctx.enter_context(tc.psum_pool(name="psum", bufs=1))
+
+        picks = lists.tile([P, S // 16], U16, name="picks")
+        places = lists.tile([P, S // 16], U16, name="places")
+
+        table_scales = keep.tile([P, T], U8, align_bytes=256, name="table_scales")
+        table_words = [keep.tile([P, T], U32, align_bytes=256, name=f"table_words{a}") for a in range(PASSES)]
+        w_raw = [keep.tile([P, PACK, M], F32, align_bytes=256, name=f"w_raw{a}") for a in range(PASSES)]
+        weights = keep.tile([P, S], F32, align_bytes=256, name="weights")
+        windows = [keep.tile([P, T], F32, align_bytes=256, name=f"window{m}") for m in range(M_TILES)]
+
+        nc.vector.memset(table_scales[:].bitcast(I32), 0)
+        nc.vector.memset(windows[0][:], 0.0)
+        nc.gpsimd.memset(windows[1][:], 0.0)
+
+        tab_words = tab.bitcast(I32)
+        nc.sync.dma_start(picks[:], offs)
+        scale_start = P * T
+        for q in range(4):
+            c0 = scale_start + q * T
+            nc.scalar.dma_start(
+                out=table_scales[32 * q : 32 * q + 4 * PASSES, :].bitcast(I32),
+                in_=tab_words[:, c0 : c0 + T].rearrange("a (r t) -> a r t", r=4),
+            )
+
+        def load_words(a):
+            nc.sync.dma_start(
+                out=table_words[a][:].bitcast(I32),
+                in_=tab_words[a, 0 : P * T].rearrange("(p t) -> p t", p=P),
+            )
+
+        def load_w(a):
+            nc.sync.dma_start(
+                out=w_raw[a][:],
+                in_=w[a * K_PASS : (a + 1) * K_PASS, :].rearrange("(p j) n -> p j n", j=PACK),
+            )
+
+        load_words(0)
+        load_words(1)
+        load_w(0)
+        load_w(1)
+        load_words(2)
+        load_w(2)
+        nc.sync.dma_start(weights[:], wgo)
+        nc.sync.dma_start(places[:], offs2)
+
+        picked_scales = keep.tile([P, S], U8, align_bytes=256, name="picked_scales")
+        picked_words = [keep.tile([P, S], U32, align_bytes=256, name=f"picked_words{a}") for a in range(PASSES)]
+        w_codes = [keep.tile([P, M], U32, align_bytes=256, name=f"w_codes{a}") for a in range(PASSES)]
+        w_scales = [keep.tile([P, M], U8, align_bytes=256, name=f"w_scales{a}") for a in range(PASSES)]
+        w_grouped = [keep.tile([P, M, PACK], BF16, align_bytes=256, name=f"w_grouped{a}") for a in range(PASSES)]
+        accs = [[psum.tile([P, HALF], F32, name=f"acc{m}{h}") for h in range(HALVES)] for m in range(M_TILES)]
+
+        def gather_words(a, h0, h1):
+            nc.vector.tensor_copy(
+                picked_words[a][:, h0 * HALF : h1 * HALF],
+                table_words[a][:].indirect(picks[:, h0 * HALF // 16 : h1 * HALF // 16]),
+            )
+
+        def interleave(a, n0, n1):
+            nc.scalar.copy(out=w_grouped[a][:, n0:n1, :], in_=w_raw[a][:, :, n0:n1].rearrange("p j n -> p n j"))
+
+        def quantize(a, n0, n1):
+            nc.vector.quantize_mx(
+                out=w_codes[a][:, n0:n1].bitcast(FP8X4),
+                scales=w_scales[a][:, n0:n1],
+                in_=w_grouped[a][:, n0:n1, :].rearrange("p n j -> p (n j)"),
+            )
+
+        def multiply(a, m, h):
+            cols = slice(h * HALF, (h + 1) * HALF)
+            nc.tensor.matmul_mx(
+                out=accs[m][h][:],
+                lhsT=w_codes[a][:, m * P : (m + 1) * P].bitcast(FP8X4),
+                lhsT_scale=w_scales[a][:, m * P : (m + 1) * P],
+                rhs=picked_words[a][:, cols].bitcast(FP8X4),
+                rhs_scale=picked_scales[4 * a : P, cols],
+                start=(a == 0),
+                stop=(a == PASSES - 1),
+            )
+
+        def scatter(m, h):
+            y = keep.tile([P, HALF], F32, name=f"y{m}{h}")
+            nc.scalar.copy(out=y[:], in_=accs[m][h][:])
+            nc.vector.tensor_tensor(
+                windows[m][:].indirect(places[:, h * HALF // 16 : (h + 1) * HALF // 16]),
+                y[:],
+                weights[:, h * HALF : (h + 1) * HALF],
+                MULT,
+            )
+
+        gather_words(0, 0, 2)
+        nc.vector.tensor_copy(picked_scales[:], table_scales[:].indirect(picks[:]))
+        gather_words(1, 0, 2)
+        for a in range(2):
+            interleave(a, 0, M)
+            quantize(a, 0, M)
+        for m in range(M_TILES):
+            for h in range(HALVES):
+                for a in range(2):
+                    multiply(a, m, h)
+        gather_words(2, 0, 1)
+        interleave(2, 0, P)
+        quantize(2, 0, P)
+        multiply(2, 0, 0)
+        gather_words(2, 1, 2)
+        interleave(2, P, M)
+        quantize(2, P, M)
+        multiply(2, 0, 1)
+        multiply(2, 1, 0)
+        multiply(2, 1, 1)
+        for m in range(M_TILES):
+            for h in range(HALVES):
+                scatter(m, h)
+            nc.sync.dma_start(out=out[m * P : (m + 1) * P, :], in_=windows[m][:])

@@ -36,21 +36,25 @@ def tile_list_tabhs_none_kernel(tc, tab, w, wgo, offs, offs2, out):
         table_scales = keep.tile([P, T], U8, align_bytes=256, name="table_scales")
         table_words = [keep.tile([P, T], U32, align_bytes=256, name=f"table_words{a}") for a in range(PASSES)]
         w_raw = [keep.tile([P, PACK, M], F32, align_bytes=256, name=f"w_raw{a}") for a in range(PASSES)]
-        weights = keep.tile([P, S], F32, align_bytes=256, name="weights")
+        weights = [keep.tile([P, HALF], F32, align_bytes=256, name=f"weights{h}") for h in range(HALVES)]
         windows = [keep.tile([P, T], F32, align_bytes=256, name=f"window{m}") for m in range(M_TILES)]
+        picked_scales = keep.tile([P, S], U8, align_bytes=256, name="picked_scales")
+        picked_words = [keep.tile([P, S], U32, align_bytes=256, name=f"picked_words{a}") for a in range(PASSES)]
+        w_codes = [keep.tile([P, M], U32, align_bytes=256, name=f"w_codes{a}") for a in range(PASSES)]
+        w_scales = [keep.tile([P, M], U8, align_bytes=256, name=f"w_scales{a}") for a in range(PASSES)]
+        w_grouped = [keep.tile([P, M, PACK], BF16, align_bytes=256, name=f"w_grouped{a}") for a in range(PASSES)]
 
-        nc.vector.memset(table_scales[:].bitcast(I32), 0)
+        nc.gpsimd.memset(table_scales[:].bitcast(I32), 0)
         nc.vector.memset(windows[0][:], 0.0)
         nc.gpsimd.memset(windows[1][:], 0.0)
 
         tab_words = tab.bitcast(I32)
-        nc.sync.dma_start(picks[:], offs)
-        scale_start = P * T
-        for q in range(4):
-            c0 = scale_start + q * T
-            nc.scalar.dma_start(
-                out=table_scales[32 * q : 32 * q + 4 * PASSES, :].bitcast(I32),
-                in_=tab_words[:, c0 : c0 + T].rearrange("a (r t) -> a r t", r=4),
+
+        def load_scales(queue, q, a0, a1):
+            c0 = P * T + q * T
+            queue.dma_start(
+                out=table_scales[32 * q + 4 * a0 : 32 * q + 4 * a1, :].bitcast(I32),
+                in_=tab_words[a0:a1, c0 : c0 + T].rearrange("a (r t) -> a r t", r=4),
             )
 
         def load_words(a):
@@ -65,81 +69,61 @@ def tile_list_tabhs_none_kernel(tc, tab, w, wgo, offs, offs2, out):
                 in_=w[a * K_PASS : (a + 1) * K_PASS, :].rearrange("(p j) n -> p j n", j=PACK),
             )
 
+        nc.sync.dma_start(picks[:], offs)
         load_words(0)
+        for q in (0, 1):
+            load_scales(nc.sync, q, 0, 2)
+            load_scales(nc.sync, q, 2, 3)
+        for q in (2, 3):
+            load_scales(nc.scalar, q, 0, 3)
         load_words(1)
-        load_w(0)
-        load_w(1)
+        for a in range(PASSES):
+            load_w(a)
         load_words(2)
-        load_w(2)
-        nc.sync.dma_start(weights[:], wgo)
         nc.sync.dma_start(places[:], offs2)
-
-        picked_scales = keep.tile([P, S], U8, align_bytes=256, name="picked_scales")
-        picked_words = [keep.tile([P, S], U32, align_bytes=256, name=f"picked_words{a}") for a in range(PASSES)]
-        w_codes = [keep.tile([P, M], U32, align_bytes=256, name=f"w_codes{a}") for a in range(PASSES)]
-        w_scales = [keep.tile([P, M], U8, align_bytes=256, name=f"w_scales{a}") for a in range(PASSES)]
-        w_grouped = [keep.tile([P, M, PACK], BF16, align_bytes=256, name=f"w_grouped{a}") for a in range(PASSES)]
-        accs = [[psum.tile([P, HALF], F32, name=f"acc{m}{h}") for h in range(HALVES)] for m in range(M_TILES)]
+        for h in range(HALVES):
+            nc.sync.dma_start(weights[h][:], wgo[:, h * HALF : (h + 1) * HALF])
 
         def gather_words(a, h0, h1):
             nc.vector.tensor_copy(
-                picked_words[a][:, h0 * HALF : h1 * HALF],
-                table_words[a][:].indirect(picks[:, h0 * HALF // 16 : h1 * HALF // 16]),
+                picked_words[a][:, h0:h1],
+                table_words[a][:].indirect(picks[:, h0 // 16 : h1 // 16]),
             )
 
-        def interleave(a, n0, n1):
-            nc.scalar.copy(out=w_grouped[a][:, n0:n1, :], in_=w_raw[a][:, :, n0:n1].rearrange("p j n -> p n j"))
-
-        def quantize(a, n0, n1):
-            nc.vector.quantize_mx(
-                out=w_codes[a][:, n0:n1].bitcast(FP8X4),
-                scales=w_scales[a][:, n0:n1],
-                in_=w_grouped[a][:, n0:n1, :].rearrange("p n j -> p (n j)"),
-            )
-
-        def multiply(a, m, h):
-            cols = slice(h * HALF, (h + 1) * HALF)
-            nc.tensor.matmul_mx(
-                out=accs[m][h][:],
-                lhsT=w_codes[a][:, m * P : (m + 1) * P].bitcast(FP8X4),
-                lhsT_scale=w_scales[a][:, m * P : (m + 1) * P],
-                rhs=picked_words[a][:, cols].bitcast(FP8X4),
-                rhs_scale=picked_scales[4 * a : P, cols],
-                start=(a == 0),
-                stop=(a == PASSES - 1),
-            )
-
-        def scatter(m, h):
-            y = keep.tile([P, HALF], F32, name=f"y{m}{h}")
-            nc.scalar.copy(out=y[:], in_=accs[m][h][:])
-            nc.vector.tensor_tensor(
-                windows[m][:].indirect(places[:, h * HALF // 16 : (h + 1) * HALF // 16]),
-                y[:],
-                weights[:, h * HALF : (h + 1) * HALF],
-                MULT,
-            )
-
-        gather_words(0, 0, 2)
+        gather_words(0, 0, S)
         nc.vector.tensor_copy(picked_scales[:], table_scales[:].indirect(picks[:]))
-        gather_words(1, 0, 2)
-        for a in range(2):
-            interleave(a, 0, M)
-            quantize(a, 0, M)
+        gather_words(1, 0, S)
+        for a in range(PASSES):
+            nc.scalar.copy(out=w_grouped[a][:], in_=w_raw[a][:].rearrange("p j n -> p n j"))
+            nc.vector.quantize_mx(
+                out=w_codes[a][:].bitcast(FP8X4),
+                scales=w_scales[a][:],
+                in_=w_grouped[a][:].rearrange("p n j -> p (n j)"),
+            )
+        gather_words(2, 0, HALF)
+        gather_words(2, HALF, S)
+
         for m in range(M_TILES):
+            rows = slice(m * P, (m + 1) * P)
             for h in range(HALVES):
-                for a in range(2):
-                    multiply(a, m, h)
-        gather_words(2, 0, 1)
-        interleave(2, 0, P)
-        quantize(2, 0, P)
-        multiply(2, 0, 0)
-        gather_words(2, 1, 2)
-        interleave(2, P, M)
-        quantize(2, P, M)
-        multiply(2, 0, 1)
-        multiply(2, 1, 0)
-        multiply(2, 1, 1)
-        for m in range(M_TILES):
-            for h in range(HALVES):
-                scatter(m, h)
-            nc.sync.dma_start(out=out[m * P : (m + 1) * P, :], in_=windows[m][:])
+                cols = slice(h * HALF, (h + 1) * HALF)
+                acc = psum.tile([P, HALF], F32)
+                for a in range(PASSES):
+                    nc.tensor.matmul_mx(
+                        out=acc[:],
+                        lhsT=w_codes[a][:, rows].bitcast(FP8X4),
+                        lhsT_scale=w_scales[a][:, rows],
+                        rhs=picked_words[a][:, cols].bitcast(FP8X4),
+                        rhs_scale=picked_scales[4 * a : P, cols],
+                        start=(a == 0),
+                        stop=(a == PASSES - 1),
+                    )
+                y = keep.tile([P, HALF], F32, name=f"y{m}{h}")
+                nc.scalar.copy(out=y[:], in_=acc[:])
+                nc.vector.tensor_tensor(
+                    windows[m][:].indirect(places[:, h * HALF // 16 : (h + 1) * HALF // 16]),
+                    y[:],
+                    weights[h][:],
+                    MULT,
+                )
+            nc.sync.dma_start(out=out[rows, :], in_=windows[m][:])

@@ -19,8 +19,17 @@ PACK = 4
 K_PASS = P * PACK
 PASSES = K // K_PASS
 M_TILES = M // P
+LIST_COLUMN = 16
+
 HALF = 512
 HALVES = S // HALF
+
+QUADRANTS = 4
+SCALE_ROWS = 4
+
+
+def list_slice(entries, start, stop):
+    return entries[:, start // LIST_COLUMN : stop // LIST_COLUMN]
 
 
 def tile_list_tabhs_none_kernel(tc, tab, w, wgo, offs, offs2, out):
@@ -30,37 +39,43 @@ def tile_list_tabhs_none_kernel(tc, tab, w, wgo, offs, offs2, out):
         keep = ctx.enter_context(tc.tile_pool(name="keep", bufs=1))
         psum = ctx.enter_context(tc.psum_pool(name="psum", bufs=1))
 
-        picks = lists.tile([P, S // 16], U16, name="picks")
-        places = lists.tile([P, S // 16], U16, name="places")
+        picks = lists.tile([P, S // LIST_COLUMN], U16, name="picks")
+        places = lists.tile([P, S // LIST_COLUMN], U16, name="places")
 
-        table_scales = keep.tile([P, T], U8, align_bytes=256, name="table_scales")
         table_words = [keep.tile([P, T], U32, align_bytes=256, name=f"table_words{a}") for a in range(PASSES)]
-        w_raw = [keep.tile([P, PACK, M], F32, align_bytes=256, name=f"w_raw{a}") for a in range(PASSES)]
-        weights = [keep.tile([P, HALF], F32, align_bytes=256, name=f"weights{h}") for h in range(HALVES)]
-        windows = [keep.tile([P, T], F32, align_bytes=256, name=f"window{m}") for m in range(M_TILES)]
-        picked_scales = keep.tile([P, S], U8, align_bytes=256, name="picked_scales")
         picked_words = [keep.tile([P, S], U32, align_bytes=256, name=f"picked_words{a}") for a in range(PASSES)]
-        w_codes = [keep.tile([P, M], U32, align_bytes=256, name=f"w_codes{a}") for a in range(PASSES)]
-        w_scales = [keep.tile([P, M], U8, align_bytes=256, name=f"w_scales{a}") for a in range(PASSES)]
-        w_grouped = [keep.tile([P, M, PACK], BF16, align_bytes=256, name=f"w_grouped{a}") for a in range(PASSES)]
+        table_scales = keep.tile([P, T], U8, align_bytes=256, name="table_scales")
+        picked_scales = keep.tile([P, S], U8, align_bytes=256, name="picked_scales")
+
+        w_raw = [keep.tile([P, PACK, M], F32, align_bytes=256, name=f"w_raw{a}") for a in range(PASSES)]
+        w_grouped = keep.tile([P, PASSES, M, PACK], BF16, align_bytes=256, name="w_grouped")
+        w_codes = keep.tile([P, PASSES, M], U32, align_bytes=256, name="w_codes")
+        w_scales = keep.tile([P, PASSES, M], U8, align_bytes=256, name="w_scales")
+
+        weights = keep.tile([P, S], F32, align_bytes=256, name="weights")
+        windows = [keep.tile([P, T], F32, align_bytes=256, name=f"window{m}") for m in range(M_TILES)]
 
         nc.gpsimd.memset(table_scales[:].bitcast(I32), 0)
         nc.vector.memset(windows[0][:], 0.0)
         nc.gpsimd.memset(windows[1][:], 0.0)
 
-        tab_words = tab.bitcast(I32)
+        tab_i32 = tab.bitcast(I32)
 
-        def load_scales(queue, q, a0, a1):
-            c0 = P * T + q * T
-            queue.dma_start(
-                out=table_scales[32 * q + 4 * a0 : 32 * q + 4 * a1, :].bitcast(I32),
-                in_=tab_words[a0:a1, c0 : c0 + T].rearrange("a (r t) -> a r t", r=4),
-            )
-
-        def load_words(a):
+        def load_table_words(a):
             nc.sync.dma_start(
                 out=table_words[a][:].bitcast(I32),
-                in_=tab_words[a, 0 : P * T].rearrange("(p t) -> p t", p=P),
+                in_=tab_i32[a, 0 : P * T].rearrange("(p t) -> p t", p=P),
+            )
+
+        def load_table_scales(queue, q, first_pass, last_pass):
+            start = 32 * q + SCALE_ROWS * first_pass
+            stop = 32 * q + SCALE_ROWS * (last_pass + 1)
+            word = P * T + q * SCALE_ROWS * T // 4
+            queue.dma_start(
+                out=table_scales[start:stop, :].bitcast(I32),
+                in_=tab_i32[first_pass : last_pass + 1, word : word + SCALE_ROWS * T // 4].rearrange(
+                    "a (r t) -> a r t", r=SCALE_ROWS
+                ),
             )
 
         def load_w(a):
@@ -70,60 +85,68 @@ def tile_list_tabhs_none_kernel(tc, tab, w, wgo, offs, offs2, out):
             )
 
         nc.sync.dma_start(picks[:], offs)
-        load_words(0)
-        for q in (0, 1):
-            load_scales(nc.sync, q, 0, 2)
-            load_scales(nc.sync, q, 2, 3)
-        for q in (2, 3):
-            load_scales(nc.scalar, q, 0, 3)
-        load_words(1)
+        load_table_words(0)
+        for q in range(QUADRANTS // 2):
+            load_table_scales(nc.sync, q, 0, 1)
+            load_table_scales(nc.sync, q, 2, 2)
+        for q in range(QUADRANTS // 2, QUADRANTS):
+            load_table_scales(nc.scalar, q, 0, 2)
+        load_table_words(1)
         for a in range(PASSES):
             load_w(a)
-        load_words(2)
+        load_table_words(2)
         nc.sync.dma_start(places[:], offs2)
-        for h in range(HALVES):
-            nc.sync.dma_start(weights[h][:], wgo[:, h * HALF : (h + 1) * HALF])
+        nc.sync.dma_start(weights[:], wgo)
 
-        def gather_words(a, h0, h1):
+        def gather_words(a, start, stop):
             nc.vector.tensor_copy(
-                picked_words[a][:, h0:h1],
-                table_words[a][:].indirect(picks[:, h0 // 16 : h1 // 16]),
+                picked_words[a][:, start:stop],
+                table_words[a][:].indirect(list_slice(picks, start, stop)),
+            )
+
+        def group_w(a):
+            nc.scalar.copy(out=w_grouped[:, a, :, :], in_=w_raw[a][:].rearrange("p j n -> p n j"))
+
+        def quantize_w(first_pass, last_pass):
+            both = slice(first_pass, last_pass + 1)
+            nc.vector.quantize_mx(
+                out=w_codes[:, both, :].rearrange("p a n -> p (a n)").bitcast(FP8X4),
+                scales=w_scales[:, both, :].rearrange("p a n -> p (a n)"),
+                in_=w_grouped[:, both, :, :].rearrange("p a n j -> p (a n j)"),
             )
 
         gather_words(0, 0, S)
         nc.vector.tensor_copy(picked_scales[:], table_scales[:].indirect(picks[:]))
         gather_words(1, 0, S)
         for a in range(PASSES):
-            nc.scalar.copy(out=w_grouped[a][:], in_=w_raw[a][:].rearrange("p j n -> p n j"))
-            nc.vector.quantize_mx(
-                out=w_codes[a][:].bitcast(FP8X4),
-                scales=w_scales[a][:],
-                in_=w_grouped[a][:].rearrange("p n j -> p (n j)"),
-            )
-        gather_words(2, 0, HALF)
-        gather_words(2, HALF, S)
+            group_w(a)
+        quantize_w(0, 1)
+        quantize_w(2, 2)
+        for h in range(HALVES):
+            gather_words(2, h * HALF, (h + 1) * HALF)
 
-        for m in range(M_TILES):
-            rows = slice(m * P, (m + 1) * P)
-            for h in range(HALVES):
-                cols = slice(h * HALF, (h + 1) * HALF)
+        for h in range(HALVES):
+            cols = slice(h * HALF, (h + 1) * HALF)
+            for m in range(M_TILES):
+                rows = slice(m * P, (m + 1) * P)
                 acc = psum.tile([P, HALF], F32)
                 for a in range(PASSES):
                     nc.tensor.matmul_mx(
                         out=acc[:],
-                        lhsT=w_codes[a][:, rows].bitcast(FP8X4),
-                        lhsT_scale=w_scales[a][:, rows],
+                        lhsT=w_codes[:, a, rows].bitcast(FP8X4),
+                        lhsT_scale=w_scales[:, a, rows],
                         rhs=picked_words[a][:, cols].bitcast(FP8X4),
-                        rhs_scale=picked_scales[4 * a : P, cols],
+                        rhs_scale=picked_scales[SCALE_ROWS * a : P, cols],
                         start=(a == 0),
                         stop=(a == PASSES - 1),
                     )
                 y = keep.tile([P, HALF], F32, name=f"y{m}{h}")
                 nc.scalar.copy(out=y[:], in_=acc[:])
                 nc.vector.tensor_tensor(
-                    windows[m][:].indirect(places[:, h * HALF // 16 : (h + 1) * HALF // 16]),
+                    windows[m][:].indirect(list_slice(places, h * HALF, (h + 1) * HALF)),
                     y[:],
-                    weights[h][:],
+                    weights[:, cols],
                     MULT,
                 )
-            nc.sync.dma_start(out=out[rows, :], in_=windows[m][:])
+        for m in range(M_TILES):
+            nc.sync.dma_start(out=out[m * P : (m + 1) * P, :], in_=windows[m][:])

from contextlib import ExitStack

import concourse.mybir as mybir

K, M, T, S = 1536, 256, 2048, 1024
FLOPS = 2 * K * M * S

F32 = mybir.dt.float32
BF16 = mybir.dt.bfloat16
I32 = mybir.dt.int32
U32 = mybir.dt.uint32
U16 = mybir.dt.uint16
U8 = mybir.dt.uint8
FP8X4 = mybir.dt.float8_e4m3fn_x4
MULT = mybir.AluOpType.mult

P = 128
PACK = 4
K_PASS = P * PACK
PASSES = K // K_PASS
M_TILES = M // P
LIST_COLUMN = 16

HALF = 512
HALVES = S // HALF

QUADRANTS = 4
SCALE_ROWS = 4


def list_slice(entries, start, stop):
    return entries[:, start // LIST_COLUMN : stop // LIST_COLUMN]


def tile_list_tabhs_none_kernel(tc, tab, w, wgo, offs, offs2, out):
    nc = tc.nc
    with ExitStack() as ctx:
        lists = ctx.enter_context(tc.tile_pool(name="lists", bufs=1))
        keep = ctx.enter_context(tc.tile_pool(name="keep", bufs=1))
        psum = ctx.enter_context(tc.psum_pool(name="psum", bufs=1))

        picks = lists.tile([P, S // LIST_COLUMN], U16, name="picks")
        places = lists.tile([P, S // LIST_COLUMN], U16, name="places")

        table_words = [keep.tile([P, T], U32, align_bytes=256, name=f"table_words{a}") for a in range(PASSES)]
        picked_words = [keep.tile([P, S], U32, align_bytes=256, name=f"picked_words{a}") for a in range(PASSES)]
        table_scales = keep.tile([P, T], U8, align_bytes=256, name="table_scales")
        picked_scales = keep.tile([P, S], U8, align_bytes=256, name="picked_scales")

        w_raw = [keep.tile([P, PACK, M], F32, align_bytes=256, name=f"w_raw{a}") for a in range(PASSES)]
        w_grouped = keep.tile([P, PASSES, M, PACK], BF16, align_bytes=256, name="w_grouped")
        w_codes = keep.tile([P, PASSES, M], U32, align_bytes=256, name="w_codes")
        w_scales = keep.tile([P, PASSES, M], U8, align_bytes=256, name="w_scales")

        weights = keep.tile([P, S], F32, align_bytes=256, name="weights")
        windows = [keep.tile([P, T], F32, align_bytes=256, name=f"window{m}") for m in range(M_TILES)]

        nc.gpsimd.memset(table_scales[:].bitcast(I32), 0)
        nc.vector.memset(windows[0][:], 0.0)
        nc.gpsimd.memset(windows[1][:], 0.0)

        tab_i32 = tab.bitcast(I32)

        def load_table_words(a):
            nc.sync.dma_start(
                out=table_words[a][:].bitcast(I32),
                in_=tab_i32[a, 0 : P * T].rearrange("(p t) -> p t", p=P),
            )

        def load_table_scales(queue, q, first_pass, last_pass):
            start = 32 * q + SCALE_ROWS * first_pass
            stop = 32 * q + SCALE_ROWS * (last_pass + 1)
            word = P * T + q * SCALE_ROWS * T // 4
            queue.dma_start(
                out=table_scales[start:stop, :].bitcast(I32),
                in_=tab_i32[first_pass : last_pass + 1, word : word + SCALE_ROWS * T // 4].rearrange(
                    "a (r t) -> a r t", r=SCALE_ROWS
                ),
            )

        def load_w(a):
            nc.sync.dma_start(
                out=w_raw[a][:],
                in_=w[a * K_PASS : (a + 1) * K_PASS, :].rearrange("(p j) n -> p j n", j=PACK),
            )

        nc.sync.dma_start(picks[:], offs)
        load_table_words(0)
        for q in range(QUADRANTS // 2):
            load_table_scales(nc.sync, q, 0, 1)
            load_table_scales(nc.sync, q, 2, 2)
        for q in range(QUADRANTS // 2, QUADRANTS):
            load_table_scales(nc.scalar, q, 0, 2)
        load_table_words(1)
        for a in range(PASSES):
            load_w(a)
        load_table_words(2)
        nc.sync.dma_start(places[:], offs2)
        nc.sync.dma_start(weights[:], wgo)

        def gather_words(a, start, stop):
            nc.vector.tensor_copy(
                picked_words[a][:, start:stop],
                table_words[a][:].indirect(list_slice(picks, start, stop)),
            )

        def group_w(a):
            nc.scalar.copy(out=w_grouped[:, a, :, :], in_=w_raw[a][:].rearrange("p j n -> p n j"))

        def quantize_w(first_pass, last_pass):
            both = slice(first_pass, last_pass + 1)
            nc.vector.quantize_mx(
                out=w_codes[:, both, :].rearrange("p a n -> p (a n)").bitcast(FP8X4),
                scales=w_scales[:, both, :].rearrange("p a n -> p (a n)"),
                in_=w_grouped[:, both, :, :].rearrange("p a n j -> p (a n j)"),
            )

        gather_words(0, 0, S)
        nc.vector.tensor_copy(picked_scales[:], table_scales[:].indirect(picks[:]))
        gather_words(1, 0, S)
        for a in range(PASSES):
            group_w(a)
        quantize_w(0, 1)
        quantize_w(2, 2)
        for h in range(HALVES):
            gather_words(2, h * HALF, (h + 1) * HALF)

        for h in range(HALVES):
            cols = slice(h * HALF, (h + 1) * HALF)
            for m in range(M_TILES):
                rows = slice(m * P, (m + 1) * P)
                acc = psum.tile([P, HALF], F32)
                for a in range(PASSES):
                    nc.tensor.matmul_mx(
                        out=acc[:],
                        lhsT=w_codes[:, a, rows].bitcast(FP8X4),
                        lhsT_scale=w_scales[:, a, rows],
                        rhs=picked_words[a][:, cols].bitcast(FP8X4),
                        rhs_scale=picked_scales[SCALE_ROWS * a : P, cols],
                        start=(a == 0),
                        stop=(a == PASSES - 1),
                    )
                y = keep.tile([P, HALF], F32, name=f"y{m}{h}")
                nc.scalar.copy(out=y[:], in_=acc[:])
                nc.vector.tensor_tensor(
                    windows[m][:].indirect(list_slice(places, h * HALF, (h + 1) * HALF)),
                    y[:],
                    weights[:, cols],
                    MULT,
                )
        for m in range(M_TILES):
            nc.sync.dma_start(out=out[m * P : (m + 1) * P, :], in_=windows[m][:])
